import numpy as np
import ml_dtypes


def mxq(x, axis, fmt="e4m3"):
    dtype, down = {"e4m3": (ml_dtypes.float8_e4m3fn, 7), "e5m2": (ml_dtypes.float8_e5m2, 14)}[fmt]
    v = np.moveaxis(np.asarray(x, np.float32).astype(ml_dtypes.bfloat16).astype(np.float64), axis, -1)
    blocks = v.reshape(v.shape[:-1] + (-1, 32))
    amax = np.abs(blocks).max(-1, keepdims=True)
    byte = np.maximum(np.where(amax > 0, np.frexp(amax)[1] - 1 + 127, 0) - down, 1)
    scale = np.exp2(byte - 127.0)
    codes = (blocks / scale).astype(np.float32).astype(dtype).astype(np.float64)
    return np.moveaxis((codes * scale).reshape(v.shape), -1, axis)


WIDE = False


def mx_kscale(k):
    if not WIDE:
        return np.ones(k)
    levels = np.array([10, -10, 5, -5, 0])
    if k % 512:
        return np.exp2(np.random.permutation(np.resize(levels, k // 32))).repeat(32)
    a = np.empty((k // 512, 16))
    for p in range(k // 512):
        a[p, :8] = np.random.permutation(np.resize(levels, 8))
        for g in range(8):
            far = levels[np.abs(levels - a[p, g]) >= 10]
            a[p, g + 8] = far[np.random.randint(len(far))]
    return np.exp2(a.ravel()).repeat(32)


BF16 = ml_dtypes.bfloat16


def bf(x):
    return np.asarray(x, np.float32).astype(BF16)


def f64(x):
    return np.asarray(x).astype(np.float64)


E2M1 = np.array([0.0, 0.5, 1.0, 1.5, 2.0, 3.0, 4.0, 6.0, -0.0, -0.5, -1.0, -1.5, -2.0, -3.0, -4.0, -6.0])


def pack_weight(w, fmt):
    k, n = w.shape
    w = f64(bf(w)).reshape(k // 32, 32, n)
    amax = np.abs(w).max(1)
    if fmt == "e4m3":
        byte = np.frexp(amax)[1] - 1 + 127 - 7
    else:
        mant, ex = np.frexp(amax / 6.0)
        byte = np.where(mant > 0.5, ex, ex - 1) + 127
    byte = np.clip(np.where(amax > 0, byte, 1), 1, 254)
    scaled = (w * np.exp2(127.0 - byte)[:, None, :]).reshape(k, n).astype(np.float32)
    by_word = np.ascontiguousarray(scaled.reshape(k // 512, 128, 4, n).transpose(0, 1, 3, 2))
    if fmt == "e4m3":
        words = by_word.astype(ml_dtypes.float8_e4m3fn).view(np.uint8)
    else:
        c = by_word.astype(ml_dtypes.float4_e2m1fn).view(np.uint8) & 0xF
        words = c[..., 0::2] | (c[..., 1::2] << 4)
    return np.ascontiguousarray(words), np.ascontiguousarray(byte.astype(np.uint8).reshape(k // 512, 16, n))


def unpack_weight(words, scales, fmt):
    g, p, n, _ = words.shape
    if fmt == "e4m3":
        vals = np.ascontiguousarray(words).view(ml_dtypes.float8_e4m3fn).astype(np.float64)
    else:
        nib = np.empty((g, p, n, 4), np.uint8)
        nib[..., 0::2] = words & 0xF
        nib[..., 1::2] = words >> 4
        vals = E2M1[nib]
    vals = vals * np.repeat(np.exp2(scales.astype(np.float64) - 127.0), 8, axis=1)[..., None]
    return vals.transpose(0, 1, 3, 2).reshape(g * 512, n)
def pack4(w):
    words, scales = pack_weight(w, "e2m1")
    return words.reshape(words.shape[0], 128, -1), scales


def unpack4(words, scales):
    return unpack_weight(words.reshape(words.shape[0], 128, -1, 2), scales, "e2m1")


def planes(Y):
    n, m = Y.shape
    b = f64(bf(Y)).reshape(n // 32, 32, m)
    amax = np.abs(b).max(1)
    byte = np.clip(np.where(amax > 0, np.frexp(amax)[1] - 1 + 127 - 7, 1), 1, 254)
    codes = (b * np.exp2(127.0 - byte)[:, None, :]).reshape(n, m).astype(np.float32).astype(ml_dtypes.float8_e4m3fn).view(np.uint8)
    words = codes.reshape(n // 512, 128, 4, m).transpose(0, 1, 3, 2)
    return np.ascontiguousarray(words), np.ascontiguousarray(byte.astype(np.uint8).reshape(n // 512, 16, m))


P, C, F = 3072, 1024, 512

def setup_inputs():
    s = mx_kscale(C)
    t = mx_kscale(F)
    size = np.exp(0.8 * np.random.randn(C))
    x = np.random.randn(P, C)
    content = size * (x + 0.5 * np.random.randn(C))
    e = np.random.randn(C, F) / np.sqrt(C)
    x_words, x_scales = pack4(x.T * s[:, None])
    e_words, e_scales = pack4(e / s[:, None])
    gain = np.exp(0.3 * np.random.randn(F)) * t
    style = np.random.randn(F, C) / np.sqrt(F) * size / t[:, None]
    shift = 0.5 * size * np.random.randn(C)
    strength = np.random.uniform(0.3, 0.9, P)
    return {"x_words": x_words, "x_scales": x_scales, "e_words": e_words, "e_scales": e_scales,
            "gain": bf(gain), "style": bf(style), "shift": bf(shift),
            "strength": bf(strength), "content": bf(content)}

def reference(x_words, x_scales, e_words, e_scales, gain, style, shift, strength, content):
    X = unpack4(x_words, x_scales)
    E = unpack4(e_words, e_scales)
    r = f64(content)
    a = f64(strength)[:, None]
    h = (X.T @ E) * f64(gain)
    z = mxq(h, 1, "e4m3") @ mxq(f64(style), 0, "e4m3")
    y = r + a * (z + f64(shift) - r)
    Y = y.T
    words, scales = planes(Y)
    return y, words, scales

@@ -1,0 +1,374 @@
+from contextlib import ExitStack
+
+import concourse.mybir as mybir
+from concourse.masks import make_identity
+
+F32 = mybir.dt.float32
+BF16 = mybir.dt.bfloat16
+I32 = mybir.dt.int32
+U32 = mybir.dt.uint32
+U16 = mybir.dt.uint16
+U8 = mybir.dt.uint8
+FP8X4 = mybir.dt.float8_e4m3fn_x4
+FP4X4 = mybir.dt.float4_e2m1fn_x4
+ALU = mybir.AluOpType
+ACT = mybir.ActivationFunctionType
+
+PIXELS, CHANNELS, LATENT = 3072, 1024, 512
+FLOPS = 2 * PIXELS * CHANNELS * LATENT * 2
+
+P = 128
+PACK = 4
+GROUP = P * PACK
+GROUPS = CHANNELS // GROUP
+CHUNK = 512
+CHUNKS = PIXELS // CHUNK
+TILES = PIXELS // P
+TILES_PER_CHUNK = CHUNK // P
+UNITS = CHUNKS * GROUPS
+STEPS = 2 * UNITS
+SHIFT_ROW = 32
+X_CODE_PARTS = [(0, 1), (1, 2), (2, CHUNKS)]
+X_SCALE_PARTS = [(0, 2), (2, CHUNKS)]
+
+
+def part_of(parts, c):
+    for n, (lo, hi) in enumerate(parts):
+        if lo <= c < hi:
+            return n, lo
+    raise ValueError(c)
+
+
+def tile_linear_style_blend_k5_kernel(
+    tc, x_words, x_scales, e_words, e_scales, gain, style, shift, strength, content, out_0, out_1, out_2
+):
+    nc = tc.nc
+    with ExitStack() as ctx:
+        keep = ctx.enter_context(tc.tile_pool(name="keep", bufs=1))
+        work = ctx.enter_context(tc.tile_pool(name="work", bufs=2))
+        psum = ctx.enter_context(tc.psum_pool(name="psum", bufs=2))
+        ctx.enter_context(tc.manual_schedule())
+
+        def load_scale_rows(plane, scales, cols):
+            for q in range(4):
+                nc.sync.dma_start(
+                    out=plane[32 * q : 32 * q + 4, :, :].bitcast(I32),
+                    in_=scales[:, 4 * q : 4 * q + 4, cols].rearrange("g r n -> r g n").bitcast(I32),
+                )
+
+        e_scale_raw = keep.tile([P, GROUPS, LATENT], U8, name="e_scale_raw", align_bytes=64)
+        nc.vector.memset(e_scale_raw[:].bitcast(I32), 0)
+        x_code = []
+        x_scale = []
+        for n, (lo, hi) in enumerate(X_CODE_PARTS):
+            x_code.append(keep.tile([P, GROUPS, 2 * CHUNK * (hi - lo)], U8, name="x_code%d" % n, align_bytes=64))
+        for n, (lo, hi) in enumerate(X_SCALE_PARTS):
+            x_scale.append(keep.tile([P, GROUPS, CHUNK * (hi - lo)], U8, name="x_scale%d" % n, align_bytes=64))
+            nc.vector.memset(x_scale[n][:].bitcast(I32), 0)
+
+        def load_x_codes(n):
+            lo, hi = X_CODE_PARTS[n]
+            nc.sync.dma_start(
+                out=x_code[n][:].bitcast(I32),
+                in_=x_words[:, :, 2 * CHUNK * lo : 2 * CHUNK * hi].rearrange("g p b -> p g b").bitcast(I32),
+            )
+
+        def load_x_scales(n):
+            lo, hi = X_SCALE_PARTS[n]
+            load_scale_rows(x_scale[n], x_scales, slice(CHUNK * lo, CHUNK * hi))
+
+        gain_sb = keep.tile([P, PACK], BF16, name="gain_sb")
+        nc.gpsimd.dma_start(out=gain_sb[:], in_=gain.rearrange("(p t) -> p t", t=PACK))
+        rows_bf = keep.tile([P, P], BF16, name="rows_bf")
+        shift_rows = slice(SHIFT_ROW, SHIFT_ROW + CHANNELS // P)
+        nc.scalar.dma_start(out=rows_bf[0:TILES, :], in_=strength.rearrange("(i p) -> i p", p=P))
+        nc.scalar.dma_start(out=rows_bf[shift_rows, :], in_=shift.rearrange("(j p) -> j p", p=P))
+        rows_f32 = keep.tile([P, P], F32, name="rows_f32")
+        nc.gpsimd.memset(rows_f32[:], 0.0)
+        ident = keep.tile([P, P], F32, name="ident")
+        make_identity(nc, ident[:])
+
+        e_code_raw = keep.tile([P, GROUPS, 2 * LATENT], U8, name="e_code_raw", align_bytes=64)
+        style_raw = []
+        for g in range(GROUPS):
+            style_raw.append(keep.tile([P, PACK, GROUP], BF16, name="style_raw%d" % g, align_bytes=64))
+
+        def load_style(g):
+            nc.sync.dma_start(
+                out=style_raw[g][:],
+                in_=style[:, GROUP * g : GROUP * (g + 1)].rearrange("(p t) c -> p t c", t=PACK),
+            )
+
+        content_sb = {}
+
+        def load_content(pair):
+            content_sb[pair] = keep.tile([P, 2, CHANNELS], BF16, name="content%d" % pair)
+            nc.sync.dma_start(
+                out=content_sb[pair][:],
+                in_=content[2 * P * pair : 2 * P * (pair + 1), :].rearrange("(i p) c -> p i c", p=P),
+            )
+
+        load_scale_rows(e_scale_raw, e_scales, slice(0, LATENT))
+        nc.sync.dma_start(out=e_code_raw[:].bitcast(I32), in_=e_words.rearrange("g p b -> p g b").bitcast(I32))
+        load_x_scales(0)
+        load_x_codes(0)
+        load_style(0)
+        load_x_codes(1)
+        load_content(0)
+        load_style(1)
+        load_content(1)
+        load_x_scales(1)
+        load_x_codes(2)
+        for pair in range(2, TILES // 2):
+            load_content(pair)
+
+        e_code = keep.tile([P, GROUPS, PACK, 2 * P], U8, name="e_code", align_bytes=64)
+        e_scale = keep.tile([P, GROUPS, PACK, P], U8, name="e_scale", align_bytes=64)
+        nc.vector.tensor_copy(
+            out=e_scale[:], in_=e_scale_raw[:].rearrange("p g (m t) -> p g t m", t=PACK)
+        )
+        nc.vector.tensor_copy(
+            out=e_code[:].bitcast(U16),
+            in_=e_code_raw[:].bitcast(U16).rearrange("p g (m t) -> p g t m", t=PACK),
+        )
+
+        cols = keep.tile([P, SHIFT_ROW + CHANNELS // P], F32, name="cols")
+        rest = keep.tile([P, TILES], F32, name="rest")
+
+        def vectors():
+            nc.scalar.copy(out=rows_f32[0:TILES, :], in_=rows_bf[0:TILES, :])
+            nc.scalar.copy(out=rows_f32[shift_rows, :], in_=rows_bf[shift_rows, :])
+            turned = psum.tile([P, GROUP], F32, name="turned", tag="xt")
+            nc.tensor.transpose(turned[:, 0:P], rows_f32[:], ident[:])
+            nc.scalar.copy(out=cols[:], in_=turned[:, 0 : SHIFT_ROW + CHANNELS // P])
+            nc.scalar.activation(out=rest[:], in_=cols[:, 0:TILES], func=ACT.Copy, scale=-1.0, bias=1.0)
+
+        style_code = keep.tile([P, CHANNELS], U32, name="style_code", align_bytes=64)
+        style_scale = keep.tile([P, CHANNELS], U8, name="style_scale", align_bytes=64)
+        style_in = {}
+
+        def style_interleave(g):
+            style_in[g] = keep.tile([P, GROUP, PACK], BF16, name="style_in%d" % g, align_bytes=64)
+            dst = style_in[g][:].rearrange("p (c i) t -> p c t i", i=4)
+            src = style_raw[g][:].rearrange("p t (c i) -> p c t i", i=4)
+            if g == 0:
+                nc.scalar.copy(out=dst, in_=src)
+            else:
+                nc.vector.tensor_copy(out=dst, in_=src)
+
+        def style_quantize(g):
+            nc.vector.quantize_mx(
+                out=style_code[:, GROUP * g : GROUP * (g + 1)].bitcast(FP8X4),
+                scales=style_scale[:, GROUP * g : GROUP * (g + 1)],
+                in_=style_in[g][:].rearrange("p c t -> p (c t)"),
+            )
+
+        h_bank = {}
+        h_in = {}
+        h_code = {}
+        h_scale = {}
+        z_bank = {}
+        u_t = {}
+        u_bank = {}
+        y_sb = {}
+        y_word = {}
+        xt_bank = {}
+        y_in = {}
+        y_scale = keep.tile([P, GROUPS, PIXELS], U8, name="y_scale", align_bytes=64)
+
+        def stage1(n):
+            c = n // TILES_PER_CHUNK
+            code_part, code_lo = part_of(X_CODE_PARTS, c)
+            scale_part, scale_lo = part_of(X_SCALE_PARTS, c)
+            m = n - code_lo * TILES_PER_CHUNK
+            ms = n - scale_lo * TILES_PER_CHUNK
+            h_bank[n] = psum.tile([P, PACK, P], F32, name="h_bank", tag="h")
+            for t in range(PACK):
+                for g in range(GROUPS):
+                    nc.tensor.matmul_mx(
+                        out=h_bank[n][:, t, :],
+                        lhsT=e_code[:, g, t, :].bitcast(FP4X4),
+                        lhsT_scale=e_scale[:, g, t, :],
+                        rhs=x_code[code_part][:, g, 2 * P * m : 2 * P * (m + 1)].bitcast(FP4X4),
+                        rhs_scale=x_scale[scale_part][:, g, P * ms : P * (ms + 1)],
+                        start=(g == 0),
+                        stop=(g == GROUPS - 1),
+                    )
+
+        def apply_gain(n):
+            c, i = divmod(n, TILES_PER_CHUNK)
+            if i == 0:
+                h_in[c] = work.tile([P, CHUNK, PACK], BF16, name="h_in", align_bytes=64)
+            nc.vector.tensor_tensor(
+                out=h_in[c][:, P * i : P * (i + 1), :],
+                in0=h_bank[n][:].rearrange("p t n -> p n t"),
+                in1=gain_sb[:].unsqueeze(1).to_broadcast([P, P, PACK]),
+                op=ALU.mult,
+            )
+
+        def quantize_h(c):
+            h_code[c] = work.tile([P, CHUNK], U32, name="h_code", align_bytes=64)
+            h_scale[c] = work.tile([P, CHUNK], U8, name="h_scale", align_bytes=64)
+            nc.vector.quantize_mx(
+                out=h_code[c][:].bitcast(FP8X4), scales=h_scale[c][:], in_=h_in[c][:].rearrange("p n t -> p (n t)")
+            )
+
+        def stage2(s, k):
+            c, g = divmod(s // 2, GROUPS)
+            j = PACK * g + 2 * (s % 2) + k
+            z_bank[s, k] = psum.tile([P, CHUNK], F32, name="z_bank", tag="z")
+            nc.tensor.matmul_mx(
+                out=z_bank[s, k][:],
+                lhsT=style_code[:, P * j : P * (j + 1)].bitcast(FP8X4),
+                lhsT_scale=style_scale[:, P * j : P * (j + 1)],
+                rhs=h_code[c][:].bitcast(FP8X4),
+                rhs_scale=h_scale[c][:],
+                start=True,
+                stop=True,
+            )
+
+        def add_shift(s, k):
+            c, g = divmod(s // 2, GROUPS)
+            j = PACK * g + 2 * (s % 2) + k
+            u_t[c, j] = work.tile([P, CHUNK], F32, name="u_t", bufs=10)
+            nc.scalar.activation(
+                out=u_t[c, j][:],
+                in_=z_bank[s, k][:],
+                func=ACT.Identity,
+                bias=cols[:, SHIFT_ROW + j : SHIFT_ROW + j + 1],
+                scale=1.0,
+            )
+
+        def scale_content(s, k):
+            c, g = divmod(s // 2, GROUPS)
+            i = 2 * (s % 2) + k
+            n = TILES_PER_CHUNK * c + i
+            if k == 0:
+                y_sb[s] = work.tile([P, 2, GROUP], F32, name="y_sb", bufs=8)
+            nc.gpsimd.tensor_scalar(
+                out=y_sb[s][:, k, :],
+                in0=content_sb[n // 2][:, k, GROUP * g : GROUP * (g + 1)],
+                scalar1=rest[:, n : n + 1],
+                scalar2=0.0,
+                op0=ALU.mult,
+                op1=ALU.add,
+            )
+
+        def turn_u(s, k):
+            c, g = divmod(s // 2, GROUPS)
+            i = 2 * (s % 2) + k
+            u_bank[s, k] = psum.tile([P, GROUP], F32, name="u_bank", tag="u")
+            for jj in range(PACK):
+                nc.tensor.transpose(
+                    u_bank[s, k][:, P * jj : P * (jj + 1)], u_t[c, PACK * g + jj][:, P * i : P * (i + 1)], ident[:]
+                )
+
+        def blend(s, k):
+            c = s // (2 * GROUPS)
+            n = TILES_PER_CHUNK * c + 2 * (s % 2) + k
+            nc.vector.scalar_tensor_tensor(
+                out=y_sb[s][:, k, :],
+                in0=u_bank[s, k][:],
+                scalar=cols[:, n : n + 1],
+                in1=y_sb[s][:, k, :],
+                op0=ALU.mult,
+                op1=ALU.add,
+            )
+
+        def store_y(s):
+            c, g = divmod(s // 2, GROUPS)
+            row = CHUNK * c + 2 * P * (s % 2)
+            nc.sync.dma_start(
+                out=out_0[row : row + 2 * P, GROUP * g : GROUP * (g + 1)].rearrange("(i p) c -> p i c", p=P),
+                in_=y_sb[s][:],
+            )
+
+        def round_y(s, k):
+            y_word[s, k] = work.tile([P, 2, P, 2], BF16, name="y_word", bufs=6, align_bytes=64)
+            src = y_sb[s][:, k, :].rearrange("q (p u e) -> q u p e", u=2, e=2)
+            if k == 0:
+                nc.gpsimd.tensor_scalar(
+                    out=y_word[s, k][:], in0=src, scalar1=1.0, scalar2=0.0, op0=ALU.mult, op1=ALU.add
+                )
+            else:
+                nc.scalar.copy(out=y_word[s, k][:], in_=src)
+
+        def turn_y(s):
+            xt_bank[s] = psum.tile([P, 2, 2, P], F32, name="xt_bank", tag="xt")
+            for k in range(2):
+                words = y_word[s, k][:].rearrange("q u p e -> q (u p e)").bitcast(F32)
+                for u in range(2):
+                    nc.tensor.transpose(xt_bank[s][:, k, u, :], words[:, P * u : P * (u + 1)], ident[:])
+
+        def gather_words(s):
+            unit, half = divmod(s, 2)
+            if half == 0:
+                y_in[unit] = work.tile([P, CHUNK * PACK], BF16, name="y_in", align_bytes=64)
+            words = y_in[unit][:].bitcast(F32).rearrange("p (h k r u) -> p h k r u", h=2, k=2, u=2)
+            nc.scalar.copy(out=words[:, half, :, :, :], in_=xt_bank[s][:].rearrange("p k u r -> p k r u"))
+
+        def quantize_y(unit):
+            c, g = divmod(unit, GROUPS)
+            y_code = work.tile([P, CHUNK], U32, name="y_code", bufs=3, align_bytes=64)
+            nc.vector.quantize_mx(
+                out=y_code[:].bitcast(FP8X4), scales=y_scale[:, g, CHUNK * c : CHUNK * (c + 1)], in_=y_in[unit][:]
+            )
+            nc.sync.dma_start(
+                out=out_1[g, :, CHUNK * c : CHUNK * (c + 1), :].rearrange("p m t -> p (m t)").bitcast(I32),
+                in_=y_code[:].bitcast(I32),
+            )
+
+        def store_scales(lo, hi):
+            for q in range(4):
+                nc.sync.dma_start(
+                    out=out_2[:, 4 * q : 4 * q + 4, lo:hi].rearrange("g r m -> r g m").bitcast(I32),
+                    in_=y_scale[32 * q : 32 * q + 4, :, lo:hi].bitcast(I32),
+                )
+
+        def live(s):
+            return 0 <= s < STEPS
+
+        vectors()
+        style_interleave(0)
+        for s in range(-7, STEPS + 3):
+            n = s + 7
+            if live(s + 2):
+                stage2(s + 2, 0)
+                stage2(s + 2, 1)
+            if n < TILES:
+                stage1(n)
+            if live(s):
+                turn_u(s, 0)
+                turn_u(s, 1)
+            if live(s - 2):
+                turn_y(s - 2)
+            if live(s - 3):
+                gather_words(s - 3)
+            if live(s + 2):
+                add_shift(s + 2, 0)
+                add_shift(s + 2, 1)
+            if live(s - 1):
+                round_y(s - 1, 0)
+                round_y(s - 1, 1)
+            if live(s + 2):
+                scale_content(s + 2, 0)
+                scale_content(s + 2, 1)
+            if n % TILES_PER_CHUNK == 0 and 0 < n <= TILES:
+                quantize_h(n // TILES_PER_CHUNK - 1)
+            if s == -3:
+                style_quantize(0)
+            if live(s - 3) and (s - 3) % 2 == 1:
+                quantize_y((s - 3) // 2)
+                if (s - 3) // 2 == UNITS - GROUPS - 1:
+                    store_scales(0, PIXELS - CHUNK)
+            if n < TILES:
+                apply_gain(n)
+            if s == -2:
+                style_interleave(1)
+            if s == -1:
+                style_quantize(1)
+            if live(s):
+                blend(s, 0)
+                blend(s, 1)
+                store_y(s)
+        store_scales(PIXELS - CHUNK, PIXELS)

@@ -21,79 +21,87 @@ P = 128
 PACK = 4
 GROUP = P * PACK
 GROUPS = CHANNELS // GROUP
-CHUNK = 512
-CHUNKS = PIXELS // CHUNK
 TILES = PIXELS // P
-TILES_PER_CHUNK = CHUNK // P
-UNITS = CHUNKS * GROUPS
-STEPS = 2 * UNITS
+PAIR = 2 * P
+PAIRS = PIXELS // PAIR
+CHUNK_PAIRS = [1, 2, 2, 2, 2, 2, 1]
+STEPS = GROUPS * PAIRS
 SHIFT_ROW = 32
-X_CODE_PARTS = [(0, 1), (1, 2), (2, CHUNKS)]
-X_SCALE_PARTS = [(0, 2), (2, CHUNKS)]
+X_CODE_PARTS = [0, 256, 768, PIXELS]
+X_SCALE_PARTS = [0, 768, PIXELS]
+STAGE1_AHEAD = 7
+HEAD_SHIFT = 1
+ROUND_ON_VECTOR = [17, 19, 21, 23]
+SCALE_ON_SCALAR = [0, 1, 2]
+STYLE1 = "G"
+SCALE_AHEAD = 4
+Y_BUFS = 10
 
 
-def part_of(parts, c):
-    for n, (lo, hi) in enumerate(parts):
-        if lo <= c < hi:
-            return n, lo
-    raise ValueError(c)
+def part_of(bounds, pixel):
+    n = max(i for i in range(len(bounds) - 1) if bounds[i] <= pixel)
+    return n, pixel - bounds[n]
 
 
 def tile_linear_style_blend_k5_kernel(
     tc, x_words, x_scales, e_words, e_scales, gain, style, shift, strength, content, out_0, out_1, out_2
 ):
     nc = tc.nc
+    first_pair = [sum(CHUNK_PAIRS[:c]) for c in range(len(CHUNK_PAIRS))]
+    steps = [(c, g, half) for c, pairs in enumerate(CHUNK_PAIRS) for g in range(GROUPS) for half in range(pairs)]
+    chunk_of_pair = [c for c, pairs in enumerate(CHUNK_PAIRS) for half in range(pairs)]
+
     with ExitStack() as ctx:
         keep = ctx.enter_context(tc.tile_pool(name="keep", bufs=1))
         work = ctx.enter_context(tc.tile_pool(name="work", bufs=2))
         psum = ctx.enter_context(tc.psum_pool(name="psum", bufs=2))
         ctx.enter_context(tc.manual_schedule())
 
-        def load_scale_rows(plane, scales, cols):
+        def load_scale_rows(plane, scales, lo, hi):
             for q in range(4):
                 nc.sync.dma_start(
                     out=plane[32 * q : 32 * q + 4, :, :].bitcast(I32),
-                    in_=scales[:, 4 * q : 4 * q + 4, cols].rearrange("g r n -> r g n").bitcast(I32),
+                    in_=scales[:, 4 * q : 4 * q + 4, lo:hi].rearrange("g r n -> r g n").bitcast(I32),
                 )
 
         e_scale_raw = keep.tile([P, GROUPS, LATENT], U8, name="e_scale_raw", align_bytes=64)
         nc.vector.memset(e_scale_raw[:].bitcast(I32), 0)
-        x_code = []
-        x_scale = []
-        for n, (lo, hi) in enumerate(X_CODE_PARTS):
-            x_code.append(keep.tile([P, GROUPS, 2 * CHUNK * (hi - lo)], U8, name="x_code%d" % n, align_bytes=64))
-        for n, (lo, hi) in enumerate(X_SCALE_PARTS):
-            x_scale.append(keep.tile([P, GROUPS, CHUNK * (hi - lo)], U8, name="x_scale%d" % n, align_bytes=64))
+        x_code = {}
+        x_scale = {}
+        for n in range(len(X_SCALE_PARTS) - 1):
+            width = X_SCALE_PARTS[n + 1] - X_SCALE_PARTS[n]
+            x_scale[n] = keep.tile([P, GROUPS, width], U8, name="x_scale%d" % n, align_bytes=64)
             nc.vector.memset(x_scale[n][:].bitcast(I32), 0)
 
         def load_x_codes(n):
-            lo, hi = X_CODE_PARTS[n]
+            lo, hi = X_CODE_PARTS[n], X_CODE_PARTS[n + 1]
+            x_code[n] = keep.tile([P, GROUPS, 2 * (hi - lo)], U8, name="x_code%d" % n, align_bytes=64)
             nc.sync.dma_start(
                 out=x_code[n][:].bitcast(I32),
-                in_=x_words[:, :, 2 * CHUNK * lo : 2 * CHUNK * hi].rearrange("g p b -> p g b").bitcast(I32),
+                in_=x_words[:, :, 2 * lo : 2 * hi].rearrange("g p b -> p g b").bitcast(I32),
             )
 
         def load_x_scales(n):
-            lo, hi = X_SCALE_PARTS[n]
-            load_scale_rows(x_scale[n], x_scales, slice(CHUNK * lo, CHUNK * hi))
+            load_scale_rows(x_scale[n], x_scales, X_SCALE_PARTS[n], X_SCALE_PARTS[n + 1])
 
         gain_sb = keep.tile([P, PACK], BF16, name="gain_sb")
         nc.gpsimd.dma_start(out=gain_sb[:], in_=gain.rearrange("(p t) -> p t", t=PACK))
         rows_bf = keep.tile([P, P], BF16, name="rows_bf")
         shift_rows = slice(SHIFT_ROW, SHIFT_ROW + CHANNELS // P)
-        nc.scalar.dma_start(out=rows_bf[0:TILES, :], in_=strength.rearrange("(i p) -> i p", p=P))
-        nc.scalar.dma_start(out=rows_bf[shift_rows, :], in_=shift.rearrange("(j p) -> j p", p=P))
+        nc.gpsimd.dma_start(out=rows_bf[0:TILES, :], in_=strength.rearrange("(i p) -> i p", p=P))
+        nc.gpsimd.dma_start(out=rows_bf[shift_rows, :], in_=shift.rearrange("(j p) -> j p", p=P))
         rows_f32 = keep.tile([P, P], F32, name="rows_f32")
         nc.gpsimd.memset(rows_f32[:], 0.0)
         ident = keep.tile([P, P], F32, name="ident")
         make_identity(nc, ident[:])
+        nc.gpsimd.tensor_copy(out=rows_f32[0:TILES, :], in_=rows_bf[0:TILES, :])
+        nc.gpsimd.tensor_copy(out=rows_f32[shift_rows, :], in_=rows_bf[shift_rows, :])
 
         e_code_raw = keep.tile([P, GROUPS, 2 * LATENT], U8, name="e_code_raw", align_bytes=64)
-        style_raw = []
-        for g in range(GROUPS):
-            style_raw.append(keep.tile([P, PACK, GROUP], BF16, name="style_raw%d" % g, align_bytes=64))
+        style_raw = {}
 
         def load_style(g):
+            style_raw[g] = keep.tile([P, PACK, GROUP], BF16, name="style_raw%d" % g, align_bytes=64)
             nc.sync.dma_start(
                 out=style_raw[g][:],
                 in_=style[:, GROUP * g : GROUP * (g + 1)].rearrange("(p t) c -> p t c", t=PACK),
@@ -105,43 +113,40 @@ def tile_linear_style_blend_k5_kernel(
             content_sb[pair] = keep.tile([P, 2, CHANNELS], BF16, name="content%d" % pair)
             nc.sync.dma_start(
                 out=content_sb[pair][:],
-                in_=content[2 * P * pair : 2 * P * (pair + 1), :].rearrange("(i p) c -> p i c", p=P),
+                in_=content[PAIR * pair : PAIR * (pair + 1), :].rearrange("(i p) c -> p i c", p=P),
             )
 
-        load_scale_rows(e_scale_raw, e_scales, slice(0, LATENT))
         nc.sync.dma_start(out=e_code_raw[:].bitcast(I32), in_=e_words.rearrange("g p b -> p g b").bitcast(I32))
-        load_x_scales(0)
+        load_scale_rows(e_scale_raw, e_scales, 0, LATENT)
         load_x_codes(0)
         load_style(0)
+        load_style(1)
+        load_x_scales(0)
         load_x_codes(1)
         load_content(0)
-        load_style(1)
         load_content(1)
+        load_content(2)
         load_x_scales(1)
         load_x_codes(2)
-        for pair in range(2, TILES // 2):
+        for pair in range(3, PAIRS):
             load_content(pair)
 
         e_code = keep.tile([P, GROUPS, PACK, 2 * P], U8, name="e_code", align_bytes=64)
         e_scale = keep.tile([P, GROUPS, PACK, P], U8, name="e_scale", align_bytes=64)
         nc.vector.tensor_copy(
-            out=e_scale[:], in_=e_scale_raw[:].rearrange("p g (m t) -> p g t m", t=PACK)
-        )
-        nc.vector.tensor_copy(
             out=e_code[:].bitcast(U16),
             in_=e_code_raw[:].bitcast(U16).rearrange("p g (m t) -> p g t m", t=PACK),
         )
+        nc.vector.tensor_copy(out=e_scale[:], in_=e_scale_raw[:].rearrange("p g (m t) -> p g t m", t=PACK))
 
-        cols = keep.tile([P, SHIFT_ROW + CHANNELS // P], F32, name="cols")
+        columns = keep.tile([P, SHIFT_ROW + CHANNELS // P], F32, name="columns")
         rest = keep.tile([P, TILES], F32, name="rest")
 
-        def vectors():
-            nc.scalar.copy(out=rows_f32[0:TILES, :], in_=rows_bf[0:TILES, :])
-            nc.scalar.copy(out=rows_f32[shift_rows, :], in_=rows_bf[shift_rows, :])
+        def turn_vectors():
             turned = psum.tile([P, GROUP], F32, name="turned", tag="xt")
             nc.tensor.transpose(turned[:, 0:P], rows_f32[:], ident[:])
-            nc.scalar.copy(out=cols[:], in_=turned[:, 0 : SHIFT_ROW + CHANNELS // P])
-            nc.scalar.activation(out=rest[:], in_=cols[:, 0:TILES], func=ACT.Copy, scale=-1.0, bias=1.0)
+            nc.scalar.copy(out=columns[:], in_=turned[:, 0 : SHIFT_ROW + CHANNELS // P])
+            nc.scalar.activation(out=rest[:], in_=columns[:, 0:TILES], func=ACT.Copy, scale=-1.0, bias=1.0)
 
         style_code = keep.tile([P, CHANNELS], U32, name="style_code", align_bytes=64)
         style_scale = keep.tile([P, CHANNELS], U8, name="style_scale", align_bytes=64)
@@ -151,10 +156,19 @@ def tile_linear_style_blend_k5_kernel(
             style_in[g] = keep.tile([P, GROUP, PACK], BF16, name="style_in%d" % g, align_bytes=64)
             dst = style_in[g][:].rearrange("p (c i) t -> p c t i", i=4)
             src = style_raw[g][:].rearrange("p t (c i) -> p c t i", i=4)
-            if g == 0:
+            if g == 0 or STYLE1 == "S":
                 nc.scalar.copy(out=dst, in_=src)
-            else:
+            elif STYLE1 == "V":
                 nc.vector.tensor_copy(out=dst, in_=src)
+            else:
+                nc.gpsimd.tensor_scalar(
+                    out=style_in[g][:],
+                    in0=style_raw[g][:].rearrange("p t c -> p c t"),
+                    scalar1=1.0,
+                    scalar2=0.0,
+                    op0=ALU.mult,
+                    op1=ALU.add,
+                )
 
         def style_quantize(g):
             nc.vector.quantize_mx(
@@ -174,14 +188,13 @@ def tile_linear_style_blend_k5_kernel(
         y_word = {}
         xt_bank = {}
         y_in = {}
-        y_scale = keep.tile([P, GROUPS, PIXELS], U8, name="y_scale", align_bytes=64)
+        tail = PIXELS - PAIR * CHUNK_PAIRS[-1]
+        y_scale = keep.tile([P, GROUPS, tail], U8, name="y_scale", align_bytes=64)
+        y_scale_tail = keep.tile([P, GROUPS, PIXELS - tail], U8, name="y_scale_tail", align_bytes=64)
 
         def stage1(n):
-            c = n // TILES_PER_CHUNK
-            code_part, code_lo = part_of(X_CODE_PARTS, c)
-            scale_part, scale_lo = part_of(X_SCALE_PARTS, c)
-            m = n - code_lo * TILES_PER_CHUNK
-            ms = n - scale_lo * TILES_PER_CHUNK
+            code_part, code_at = part_of(X_CODE_PARTS, P * n)
+            scale_part, scale_at = part_of(X_SCALE_PARTS, P * n)
             h_bank[n] = psum.tile([P, PACK, P], F32, name="h_bank", tag="h")
             for t in range(PACK):
                 for g in range(GROUPS):
@@ -189,16 +202,17 @@ def tile_linear_style_blend_k5_kernel(
                         out=h_bank[n][:, t, :],
                         lhsT=e_code[:, g, t, :].bitcast(FP4X4),
                         lhsT_scale=e_scale[:, g, t, :],
-                        rhs=x_code[code_part][:, g, 2 * P * m : 2 * P * (m + 1)].bitcast(FP4X4),
-                        rhs_scale=x_scale[scale_part][:, g, P * ms : P * (ms + 1)],
+                        rhs=x_code[code_part][:, g, 2 * code_at : 2 * (code_at + P)].bitcast(FP4X4),
+                        rhs_scale=x_scale[scale_part][:, g, scale_at : scale_at + P],
                         start=(g == 0),
                         stop=(g == GROUPS - 1),
                     )
 
         def apply_gain(n):
-            c, i = divmod(n, TILES_PER_CHUNK)
+            c = chunk_of_pair[n // 2]
+            i = n - 2 * first_pair[c]
             if i == 0:
-                h_in[c] = work.tile([P, CHUNK, PACK], BF16, name="h_in", align_bytes=64)
+                h_in[c] = work.tile([P, PAIR * CHUNK_PAIRS[c], PACK], BF16, name="h_in", align_bytes=64)
             nc.vector.tensor_tensor(
                 out=h_in[c][:, P * i : P * (i + 1), :],
                 in0=h_bank[n][:].rearrange("p t n -> p n t"),
@@ -207,168 +221,184 @@ def tile_linear_style_blend_k5_kernel(
             )
 
         def quantize_h(c):
-            h_code[c] = work.tile([P, CHUNK], U32, name="h_code", align_bytes=64)
-            h_scale[c] = work.tile([P, CHUNK], U8, name="h_scale", align_bytes=64)
+            width = PAIR * CHUNK_PAIRS[c]
+            h_code[c] = work.tile([P, width], U32, name="h_code", align_bytes=64)
+            h_scale[c] = work.tile([P, width], U8, name="h_scale", align_bytes=64)
             nc.vector.quantize_mx(
                 out=h_code[c][:].bitcast(FP8X4), scales=h_scale[c][:], in_=h_in[c][:].rearrange("p n t -> p (n t)")
             )
 
-        def stage2(s, k):
-            c, g = divmod(s // 2, GROUPS)
-            j = PACK * g + 2 * (s % 2) + k
-            z_bank[s, k] = psum.tile([P, CHUNK], F32, name="z_bank", tag="z")
-            nc.tensor.matmul_mx(
-                out=z_bank[s, k][:],
-                lhsT=style_code[:, P * j : P * (j + 1)].bitcast(FP8X4),
-                lhsT_scale=style_scale[:, P * j : P * (j + 1)],
-                rhs=h_code[c][:].bitcast(FP8X4),
-                rhs_scale=h_scale[c][:],
-                start=True,
-                stop=True,
-            )
+        def channel_tiles(s):
+            c, g, half = steps[s]
+            count = PACK // CHUNK_PAIRS[c]
+            return [PACK * g + count * half + k for k in range(count)]
 
-        def add_shift(s, k):
-            c, g = divmod(s // 2, GROUPS)
-            j = PACK * g + 2 * (s % 2) + k
-            u_t[c, j] = work.tile([P, CHUNK], F32, name="u_t", bufs=10)
-            nc.scalar.activation(
-                out=u_t[c, j][:],
-                in_=z_bank[s, k][:],
-                func=ACT.Identity,
-                bias=cols[:, SHIFT_ROW + j : SHIFT_ROW + j + 1],
-                scale=1.0,
-            )
-
-        def scale_content(s, k):
-            c, g = divmod(s // 2, GROUPS)
-            i = 2 * (s % 2) + k
-            n = TILES_PER_CHUNK * c + i
-            if k == 0:
-                y_sb[s] = work.tile([P, 2, GROUP], F32, name="y_sb", bufs=8)
-            nc.gpsimd.tensor_scalar(
-                out=y_sb[s][:, k, :],
-                in0=content_sb[n // 2][:, k, GROUP * g : GROUP * (g + 1)],
-                scalar1=rest[:, n : n + 1],
-                scalar2=0.0,
-                op0=ALU.mult,
-                op1=ALU.add,
-            )
-
-        def turn_u(s, k):
-            c, g = divmod(s // 2, GROUPS)
-            i = 2 * (s % 2) + k
-            u_bank[s, k] = psum.tile([P, GROUP], F32, name="u_bank", tag="u")
-            for jj in range(PACK):
-                nc.tensor.transpose(
-                    u_bank[s, k][:, P * jj : P * (jj + 1)], u_t[c, PACK * g + jj][:, P * i : P * (i + 1)], ident[:]
+        def stage2(s):
+            c = steps[s][0]
+            width = PAIR * CHUNK_PAIRS[c]
+            per_bank = GROUP // width
+            for k, j in enumerate(channel_tiles(s)):
+                if k % per_bank == 0:
+                    bank = psum.tile([P, per_bank, width], F32, name="bank", tag="z")
+                z_bank[c, j] = bank[:, k % per_bank, :]
+                nc.tensor.matmul_mx(
+                    out=z_bank[c, j],
+                    lhsT=style_code[:, P * j : P * (j + 1)].bitcast(FP8X4),
+                    lhsT_scale=style_scale[:, P * j : P * (j + 1)],
+                    rhs=h_code[c][:].bitcast(FP8X4),
+                    rhs_scale=h_scale[c][:],
+                    start=True,
+                    stop=True,
                 )
 
-        def blend(s, k):
-            c = s // (2 * GROUPS)
-            n = TILES_PER_CHUNK * c + 2 * (s % 2) + k
-            nc.vector.scalar_tensor_tensor(
-                out=y_sb[s][:, k, :],
-                in0=u_bank[s, k][:],
-                scalar=cols[:, n : n + 1],
-                in1=y_sb[s][:, k, :],
-                op0=ALU.mult,
-                op1=ALU.add,
-            )
+        def add_shift(s):
+            c = steps[s][0]
+            for j in channel_tiles(s):
+                u_t[c, j] = work.tile([P, PAIR * CHUNK_PAIRS[c]], F32, name="u_t", bufs=10)
+                nc.scalar.activation(
+                    out=u_t[c, j][:],
+                    in_=z_bank[c, j],
+                    func=ACT.Identity,
+                    bias=columns[:, SHIFT_ROW + j : SHIFT_ROW + j + 1],
+                    scale=1.0,
+                )
 
-        def store_y(s):
-            c, g = divmod(s // 2, GROUPS)
-            row = CHUNK * c + 2 * P * (s % 2)
+        def scale_content(s):
+            c, g, half = steps[s]
+            pair = first_pair[c] + half
+            y_sb[s] = work.tile([P, 2, GROUP], F32, name="y_sb", bufs=Y_BUFS)
+            for k in range(2):
+                n = 2 * pair + k
+                src = content_sb[pair][:, k, GROUP * g : GROUP * (g + 1)]
+                if s in SCALE_ON_SCALAR:
+                    nc.scalar.activation(out=y_sb[s][:, k, :], in_=src, func=ACT.Copy, scale=rest[:, n : n + 1])
+                else:
+                    nc.vector.tensor_scalar(
+                        out=y_sb[s][:, k, :], in0=src, scalar1=rest[:, n : n + 1], scalar2=None, op0=ALU.mult
+                    )
+
+        def turn_u(s):
+            c, g, half = steps[s]
+            for k in range(2):
+                at = PAIR * half + P * k
+                u_bank[s, k] = psum.tile([P, GROUP], F32, name="u_bank", tag="u")
+                for jj in range(PACK):
+                    nc.tensor.transpose(
+                        u_bank[s, k][:, P * jj : P * (jj + 1)], u_t[c, PACK * g + jj][:, at : at + P], ident[:]
+                    )
+
+        def blend(s):
+            c, g, half = steps[s]
+            pair = first_pair[c] + half
+            for k in range(2):
+                n = 2 * pair + k
+                nc.vector.scalar_tensor_tensor(
+                    out=y_sb[s][:, k, :],
+                    in0=u_bank[s, k][:],
+                    scalar=columns[:, n : n + 1],
+                    in1=y_sb[s][:, k, :],
+                    op0=ALU.mult,
+                    op1=ALU.add,
+                )
             nc.sync.dma_start(
-                out=out_0[row : row + 2 * P, GROUP * g : GROUP * (g + 1)].rearrange("(i p) c -> p i c", p=P),
+                out=out_0[PAIR * pair : PAIR * (pair + 1), GROUP * g : GROUP * (g + 1)].rearrange(
+                    "(i p) c -> p i c", p=P
+                ),
                 in_=y_sb[s][:],
             )
 
-        def round_y(s, k):
-            y_word[s, k] = work.tile([P, 2, P, 2], BF16, name="y_word", bufs=6, align_bytes=64)
-            src = y_sb[s][:, k, :].rearrange("q (p u e) -> q u p e", u=2, e=2)
-            if k == 0:
-                nc.gpsimd.tensor_scalar(
-                    out=y_word[s, k][:], in0=src, scalar1=1.0, scalar2=0.0, op0=ALU.mult, op1=ALU.add
-                )
+        def round_y(s):
+            y_word[s] = work.tile([P, 2, PAIR, 2], BF16, name="y_word", bufs=3, align_bytes=64)
+            src = y_sb[s][:].rearrange("q k c -> q (k c)").rearrange("q (w u e) -> q u w e", u=2, e=2)
+            if s in ROUND_ON_VECTOR:
+                nc.vector.tensor_copy(out=y_word[s][:], in_=src)
             else:
-                nc.scalar.copy(out=y_word[s, k][:], in_=src)
+                nc.scalar.copy(out=y_word[s][:], in_=src)
 
         def turn_y(s):
             xt_bank[s] = psum.tile([P, 2, 2, P], F32, name="xt_bank", tag="xt")
-            for k in range(2):
-                words = y_word[s, k][:].rearrange("q u p e -> q (u p e)").bitcast(F32)
-                for u in range(2):
-                    nc.tensor.transpose(xt_bank[s][:, k, u, :], words[:, P * u : P * (u + 1)], ident[:])
+            words = y_word[s][:].rearrange("q u w e -> q (u w e)").bitcast(F32)
+            for u in range(2):
+                for k in range(2):
+                    at = P * (2 * u + k)
+                    nc.tensor.transpose(xt_bank[s][:, k, u, :], words[:, at : at + P], ident[:])
 
         def gather_words(s):
-            unit, half = divmod(s, 2)
+            c, g, half = steps[s]
             if half == 0:
-                y_in[unit] = work.tile([P, CHUNK * PACK], BF16, name="y_in", align_bytes=64)
-            words = y_in[unit][:].bitcast(F32).rearrange("p (h k r u) -> p h k r u", h=2, k=2, u=2)
+                y_in[c, g] = work.tile([P, PAIR * CHUNK_PAIRS[c] * PACK], BF16, name="y_in", bufs=3, align_bytes=64)
+            words = y_in[c, g][:].bitcast(F32).rearrange("p (h k r u) -> p h k r u", k=2, r=P, u=2)
             nc.scalar.copy(out=words[:, half, :, :, :], in_=xt_bank[s][:].rearrange("p k u r -> p k r u"))
 
-        def quantize_y(unit):
-            c, g = divmod(unit, GROUPS)
-            y_code = work.tile([P, CHUNK], U32, name="y_code", bufs=3, align_bytes=64)
-            nc.vector.quantize_mx(
-                out=y_code[:].bitcast(FP8X4), scales=y_scale[:, g, CHUNK * c : CHUNK * (c + 1)], in_=y_in[unit][:]
-            )
+        def quantize_y(s):
+            c, g, half = steps[s]
+            lo = PAIR * first_pair[c]
+            hi = lo + PAIR * CHUNK_PAIRS[c]
+            y_code = work.tile([P, hi - lo], U32, name="y_code", bufs=4, align_bytes=64)
+            plane = y_scale[:, g, lo:hi] if lo < tail else y_scale_tail[:, g, :]
+            nc.vector.quantize_mx(out=y_code[:].bitcast(FP8X4), scales=plane, in_=y_in[c, g][:])
             nc.sync.dma_start(
-                out=out_1[g, :, CHUNK * c : CHUNK * (c + 1), :].rearrange("p m t -> p (m t)").bitcast(I32),
-                in_=y_code[:].bitcast(I32),
+                out=out_1[g, :, lo:hi, :].rearrange("p m t -> p (m t)").bitcast(I32), in_=y_code[:].bitcast(I32)
             )
+            if g == GROUPS - 1 and c == len(CHUNK_PAIRS) - 2:
+                store_scales(y_scale, 0, hi)
+            if g == GROUPS - 1 and c == len(CHUNK_PAIRS) - 1:
+                store_scales(y_scale_tail, lo, hi)
 
-        def store_scales(lo, hi):
+        def store_scales(plane, lo, hi):
             for q in range(4):
                 nc.sync.dma_start(
                     out=out_2[:, 4 * q : 4 * q + 4, lo:hi].rearrange("g r m -> r g m").bitcast(I32),
-                    in_=y_scale[32 * q : 32 * q + 4, :, lo:hi].bitcast(I32),
+                    in_=plane[32 * q : 32 * q + 4, :, :].bitcast(I32),
                 )
 
-        def live(s):
-            return 0 <= s < STEPS
+        def slot_of(s):
+            return s - HEAD_SHIFT if steps[s][0] == 0 else s
 
-        vectors()
+        def at_slot(slot):
+            return [s for s in range(STEPS) if slot_of(s) == slot]
+
         style_interleave(0)
-        for s in range(-7, STEPS + 3):
-            n = s + 7
-            if live(s + 2):
-                stage2(s + 2, 0)
-                stage2(s + 2, 1)
+        if STYLE1 != "V":
+            style_interleave(1)
+        for slot in range(-STAGE1_AHEAD, STEPS + 3):
+            n = slot + STAGE1_AHEAD
+            for s in at_slot(slot + 2):
+                stage2(s)
             if n < TILES:
                 stage1(n)
-            if live(s):
-                turn_u(s, 0)
-                turn_u(s, 1)
-            if live(s - 2):
-                turn_y(s - 2)
-            if live(s - 3):
-                gather_words(s - 3)
-            if live(s + 2):
-                add_shift(s + 2, 0)
-                add_shift(s + 2, 1)
-            if live(s - 1):
-                round_y(s - 1, 0)
-                round_y(s - 1, 1)
-            if live(s + 2):
-                scale_content(s + 2, 0)
-                scale_content(s + 2, 1)
-            if n % TILES_PER_CHUNK == 0 and 0 < n <= TILES:
-                quantize_h(n // TILES_PER_CHUNK - 1)
-            if s == -3:
+            if n == 1:
+                turn_vectors()
+                for s in SCALE_ON_SCALAR:
+                    scale_content(s)
+            for s in at_slot(slot):
+                turn_u(s)
+            for s in at_slot(slot - 2):
+                turn_y(s)
+            for s in at_slot(slot - 3):
+                gather_words(s)
+            for s in at_slot(slot + 2):
+                add_shift(s)
+            for s in at_slot(slot - 1):
+                if s not in ROUND_ON_VECTOR:
+                    round_y(s)
+            if n == 2 * CHUNK_PAIRS[0]:
                 style_quantize(0)
-            if live(s - 3) and (s - 3) % 2 == 1:
-                quantize_y((s - 3) // 2)
-                if (s - 3) // 2 == UNITS - GROUPS - 1:
-                    store_scales(0, PIXELS - CHUNK)
+            if 0 < n <= TILES and n % 2 == 0 and (n == TILES or n // 2 in first_pair):
+                quantize_h(chunk_of_pair[n // 2 - 1])
+            for s in at_slot(slot - 1):
+                if s in ROUND_ON_VECTOR:
+                    round_y(s)
+            if 0 <= slot + SCALE_AHEAD < STEPS and slot + SCALE_AHEAD not in SCALE_ON_SCALAR:
+                scale_content(slot + SCALE_AHEAD)
             if n < TILES:
                 apply_gain(n)
-            if s == -2:
+            if slot == slot_of(0) - 3 and STYLE1 == "V":
                 style_interleave(1)
-            if s == -1:
+            if slot == slot_of(0) - 2:
                 style_quantize(1)
-            if live(s):
-                blend(s, 0)
-                blend(s, 1)
-                store_y(s)
-        store_scales(PIXELS - CHUNK, PIXELS)
+            for s in at_slot(slot):
+                blend(s)
+            for s in at_slot(slot - 3):
+                if steps[s][2] == CHUNK_PAIRS[steps[s][0]] - 1:
+                    quantize_y(s)

@@ -31,11 +31,12 @@ X_CODE_PARTS = [0, 256, 768, PIXELS]
 X_SCALE_PARTS = [0, 768, PIXELS]
 STAGE1_AHEAD = 7
 HEAD_SHIFT = 1
-ROUND_ON_VECTOR = [17, 19, 21, 23]
-SCALE_ON_SCALAR = [0, 1, 2]
-STYLE1 = "G"
-SCALE_AHEAD = 4
-Y_BUFS = 10
+ROUND_ON_VECTOR = [23]
+GATHER_ALL_FROM = 14
+GATHER_EVERY = 2
+GATHER_ALL_TO = 20
+SCALE_AHEAD = 2
+Y_BUFS = 6
 
 
 def part_of(bounds, pixel):
@@ -139,6 +140,7 @@ def tile_linear_style_blend_k5_kernel(
         )
         nc.vector.tensor_copy(out=e_scale[:], in_=e_scale_raw[:].rearrange("p g (m t) -> p g t m", t=PACK))
 
+        gain_wide = keep.tile([P, P // 2, PACK, 2], F32, name="gain_wide")
         columns = keep.tile([P, SHIFT_ROW + CHANNELS // P], F32, name="columns")
         rest = keep.tile([P, TILES], F32, name="rest")
 
@@ -146,7 +148,6 @@ def tile_linear_style_blend_k5_kernel(
             turned = psum.tile([P, GROUP], F32, name="turned", tag="xt")
             nc.tensor.transpose(turned[:, 0:P], rows_f32[:], ident[:])
             nc.scalar.copy(out=columns[:], in_=turned[:, 0 : SHIFT_ROW + CHANNELS // P])
-            nc.scalar.activation(out=rest[:], in_=columns[:, 0:TILES], func=ACT.Copy, scale=-1.0, bias=1.0)
 
         style_code = keep.tile([P, CHANNELS], U32, name="style_code", align_bytes=64)
         style_scale = keep.tile([P, CHANNELS], U8, name="style_scale", align_bytes=64)
@@ -156,19 +157,10 @@ def tile_linear_style_blend_k5_kernel(
             style_in[g] = keep.tile([P, GROUP, PACK], BF16, name="style_in%d" % g, align_bytes=64)
             dst = style_in[g][:].rearrange("p (c i) t -> p c t i", i=4)
             src = style_raw[g][:].rearrange("p t (c i) -> p c t i", i=4)
-            if g == 0 or STYLE1 == "S":
-                nc.scalar.copy(out=dst, in_=src)
-            elif STYLE1 == "V":
+            if g == 0:
                 nc.vector.tensor_copy(out=dst, in_=src)
             else:
-                nc.gpsimd.tensor_scalar(
-                    out=style_in[g][:],
-                    in0=style_raw[g][:].rearrange("p t c -> p c t"),
-                    scalar1=1.0,
-                    scalar2=0.0,
-                    op0=ALU.mult,
-                    op1=ALU.add,
-                )
+                nc.scalar.copy(out=dst, in_=src)
 
         def style_quantize(g):
             nc.vector.quantize_mx(
@@ -185,6 +177,7 @@ def tile_linear_style_blend_k5_kernel(
         u_t = {}
         u_bank = {}
         y_sb = {}
+        y_rows = {}
         y_word = {}
         xt_bank = {}
         y_in = {}
@@ -214,9 +207,9 @@ def tile_linear_style_blend_k5_kernel(
             if i == 0:
                 h_in[c] = work.tile([P, PAIR * CHUNK_PAIRS[c], PACK], BF16, name="h_in", align_bytes=64)
             nc.vector.tensor_tensor(
-                out=h_in[c][:, P * i : P * (i + 1), :],
-                in0=h_bank[n][:].rearrange("p t n -> p n t"),
-                in1=gain_sb[:].unsqueeze(1).to_broadcast([P, P, PACK]),
+                out=h_in[c][:, P * i : P * (i + 1), :].rearrange("p (m i) t -> p m t i", i=2),
+                in0=h_bank[n][:].rearrange("p t (m i) -> p m t i", i=2),
+                in1=gain_wide[:],
                 op=ALU.mult,
             )
 
@@ -263,19 +256,21 @@ def tile_linear_style_blend_k5_kernel(
                     scale=1.0,
                 )
 
-        def scale_content(s):
-            c, g, half = steps[s]
-            pair = first_pair[c] + half
-            y_sb[s] = work.tile([P, 2, GROUP], F32, name="y_sb", bufs=Y_BUFS)
+        def scale_content(pair):
+            y_pair = work.tile([P, GROUPS, 2, GROUP], F32, name="y_pair", bufs=Y_BUFS)
             for k in range(2):
                 n = 2 * pair + k
-                src = content_sb[pair][:, k, GROUP * g : GROUP * (g + 1)]
-                if s in SCALE_ON_SCALAR:
-                    nc.scalar.activation(out=y_sb[s][:, k, :], in_=src, func=ACT.Copy, scale=rest[:, n : n + 1])
-                else:
-                    nc.vector.tensor_scalar(
-                        out=y_sb[s][:, k, :], in0=src, scalar1=rest[:, n : n + 1], scalar2=None, op0=ALU.mult
-                    )
+                nc.gpsimd.tensor_scalar(
+                    out=y_pair[:, :, k, :],
+                    in0=content_sb[pair][:, k, :].rearrange("p (g c) -> p g c", g=GROUPS),
+                    scalar1=rest[:, n : n + 1],
+                    scalar2=0.0,
+                    op0=ALU.mult,
+                    op1=ALU.add,
+                )
+            y_rows[pair] = y_pair
+            for g in range(GROUPS):
+                y_sb[pair, g] = y_pair[:, g, :, :]
 
         def turn_u(s):
             c, g, half = steps[s]
@@ -293,23 +288,23 @@ def tile_linear_style_blend_k5_kernel(
             for k in range(2):
                 n = 2 * pair + k
                 nc.vector.scalar_tensor_tensor(
-                    out=y_sb[s][:, k, :],
+                    out=y_sb[pair, g][:, k, :],
                     in0=u_bank[s, k][:],
                     scalar=columns[:, n : n + 1],
-                    in1=y_sb[s][:, k, :],
+                    in1=y_sb[pair, g][:, k, :],
                     op0=ALU.mult,
                     op1=ALU.add,
                 )
-            nc.sync.dma_start(
-                out=out_0[PAIR * pair : PAIR * (pair + 1), GROUP * g : GROUP * (g + 1)].rearrange(
-                    "(i p) c -> p i c", p=P
-                ),
-                in_=y_sb[s][:],
-            )
+                if g == GROUPS - 1:
+                    nc.sync.dma_start(
+                        out=out_0[P * n : P * (n + 1), :].rearrange("p (g c) -> p g c", g=GROUPS),
+                        in_=y_rows[pair][:, :, k, :],
+                    )
 
         def round_y(s):
             y_word[s] = work.tile([P, 2, PAIR, 2], BF16, name="y_word", bufs=3, align_bytes=64)
-            src = y_sb[s][:].rearrange("q k c -> q (k c)").rearrange("q (w u e) -> q u w e", u=2, e=2)
+            c, g, half = steps[s]
+            src = y_sb[first_pair[c] + half, g].rearrange("q k c -> q (k c)").rearrange("q (w u e) -> q u w e", u=2, e=2)
             if s in ROUND_ON_VECTOR:
                 nc.vector.tensor_copy(out=y_word[s][:], in_=src)
             else:
@@ -328,7 +323,11 @@ def tile_linear_style_blend_k5_kernel(
             if half == 0:
                 y_in[c, g] = work.tile([P, PAIR * CHUNK_PAIRS[c] * PACK], BF16, name="y_in", bufs=3, align_bytes=64)
             words = y_in[c, g][:].bitcast(F32).rearrange("p (h k r u) -> p h k r u", k=2, r=P, u=2)
-            nc.scalar.copy(out=words[:, half, :, :, :], in_=xt_bank[s][:].rearrange("p k u r -> p k r u"))
+            src = xt_bank[s][:].rearrange("p k u r -> p k r u")
+            if gather_on_vector(s):
+                nc.vector.tensor_copy(out=words[:, half, :, :, :], in_=src)
+            else:
+                nc.scalar.copy(out=words[:, half, :, :, :], in_=src)
 
         def quantize_y(s):
             c, g, half = steps[s]
@@ -352,6 +351,9 @@ def tile_linear_style_blend_k5_kernel(
                     in_=plane[32 * q : 32 * q + 4, :, :].bitcast(I32),
                 )
 
+        def gather_on_vector(s):
+            return s < GATHER_ALL_TO and (s % GATHER_EVERY == 0 or s >= GATHER_ALL_FROM)
+
         def slot_of(s):
             return s - HEAD_SHIFT if steps[s][0] == 0 else s
 
@@ -359,8 +361,11 @@ def tile_linear_style_blend_k5_kernel(
             return [s for s in range(STEPS) if slot_of(s) == slot]
 
         style_interleave(0)
-        if STYLE1 != "V":
-            style_interleave(1)
+        style_interleave(1)
+        nc.vector.tensor_copy(
+            out=gain_wide[:], in_=gain_sb[:].unsqueeze(1).unsqueeze(3).to_broadcast([P, P // 2, PACK, 2])
+        )
+        style_quantize(0)
         for slot in range(-STAGE1_AHEAD, STEPS + 3):
             n = slot + STAGE1_AHEAD
             for s in at_slot(slot + 2):
@@ -369,33 +374,34 @@ def tile_linear_style_blend_k5_kernel(
                 stage1(n)
             if n == 1:
                 turn_vectors()
-                for s in SCALE_ON_SCALAR:
-                    scale_content(s)
             for s in at_slot(slot):
                 turn_u(s)
             for s in at_slot(slot - 2):
                 turn_y(s)
             for s in at_slot(slot - 3):
-                gather_words(s)
+                if not gather_on_vector(s):
+                    gather_words(s)
             for s in at_slot(slot + 2):
                 add_shift(s)
+                if s == 0:
+                    nc.scalar.activation(out=rest[:], in_=columns[:, 0:TILES], func=ACT.Copy, scale=-1.0, bias=1.0)
             for s in at_slot(slot - 1):
                 if s not in ROUND_ON_VECTOR:
                     round_y(s)
-            if n == 2 * CHUNK_PAIRS[0]:
-                style_quantize(0)
             if 0 < n <= TILES and n % 2 == 0 and (n == TILES or n // 2 in first_pair):
                 quantize_h(chunk_of_pair[n // 2 - 1])
             for s in at_slot(slot - 1):
                 if s in ROUND_ON_VECTOR:
                     round_y(s)
-            if 0 <= slot + SCALE_AHEAD < STEPS and slot + SCALE_AHEAD not in SCALE_ON_SCALAR:
-                scale_content(slot + SCALE_AHEAD)
+            for s in at_slot(slot + SCALE_AHEAD):
+                if steps[s][1] == 0:
+                    scale_content(first_pair[steps[s][0]] + steps[s][2])
+            for s in at_slot(slot - 3):
+                if gather_on_vector(s):
+                    gather_words(s)
             if n < TILES:
                 apply_gain(n)
-            if slot == slot_of(0) - 3 and STYLE1 == "V":
-                style_interleave(1)
-            if slot == slot_of(0) - 2:
+            if slot == slot_of(0) - 3:
                 style_quantize(1)
             for s in at_slot(slot):
                 blend(s)

@@ -24,19 +24,19 @@ GROUPS = CHANNELS // GROUP
 TILES = PIXELS // P
 PAIR = 2 * P
 PAIRS = PIXELS // PAIR
-CHUNK_PAIRS = [1, 2, 2, 2, 2, 2, 1]
+CHUNK_PAIRS = [1, 1, 2, 2, 2, 2, 2]
 STEPS = GROUPS * PAIRS
 SHIFT_ROW = 32
-X_CODE_PARTS = [0, 256, 768, PIXELS]
-X_SCALE_PARTS = [0, 768, PIXELS]
-STAGE1_AHEAD = 7
-HEAD_SHIFT = 1
+X_CODE_PARTS = [0, 256, 1024, PIXELS]
+X_SCALE_PARTS = [0, 1024, PIXELS]
 ROUND_ON_VECTOR = [23]
-GATHER_ALL_FROM = 14
-GATHER_EVERY = 2
-GATHER_ALL_TO = 20
+GATHER_ALL_FROM = 16
+GATHER_ALL_TO = 19
 SCALE_AHEAD = 2
-Y_BUFS = 6
+REST_SLOT = -2
+FINE_TAIL = 1
+BANKS = {"h": 2, "z": 2, "u": 2, "xt": 2}
+Y_BUFS = 5
 
 
 def part_of(bounds, pixel):
@@ -86,7 +86,6 @@ def tile_linear_style_blend_k5_kernel(
             load_scale_rows(x_scale[n], x_scales, X_SCALE_PARTS[n], X_SCALE_PARTS[n + 1])
 
         gain_sb = keep.tile([P, PACK], BF16, name="gain_sb")
-        nc.gpsimd.dma_start(out=gain_sb[:], in_=gain.rearrange("(p t) -> p t", t=PACK))
         rows_bf = keep.tile([P, P], BF16, name="rows_bf")
         shift_rows = slice(SHIFT_ROW, SHIFT_ROW + CHANNELS // P)
         nc.gpsimd.dma_start(out=rows_bf[0:TILES, :], in_=strength.rearrange("(i p) -> i p", p=P))
@@ -95,8 +94,8 @@ def tile_linear_style_blend_k5_kernel(
         nc.gpsimd.memset(rows_f32[:], 0.0)
         ident = keep.tile([P, P], F32, name="ident")
         make_identity(nc, ident[:])
-        nc.gpsimd.tensor_copy(out=rows_f32[0:TILES, :], in_=rows_bf[0:TILES, :])
-        nc.gpsimd.tensor_copy(out=rows_f32[shift_rows, :], in_=rows_bf[shift_rows, :])
+        nc.scalar.copy(out=rows_f32[0:TILES, :], in_=rows_bf[0:TILES, :])
+        nc.scalar.copy(out=rows_f32[shift_rows, :], in_=rows_bf[shift_rows, :])
 
         e_code_raw = keep.tile([P, GROUPS, 2 * LATENT], U8, name="e_code_raw", align_bytes=64)
         style_raw = {}
@@ -121,8 +120,9 @@ def tile_linear_style_blend_k5_kernel(
         load_scale_rows(e_scale_raw, e_scales, 0, LATENT)
         load_x_codes(0)
         load_style(0)
-        load_style(1)
+        nc.sync.dma_start(out=gain_sb[:], in_=gain.rearrange("(p t) -> p t", t=PACK))
         load_x_scales(0)
+        load_style(1)
         load_x_codes(1)
         load_content(0)
         load_content(1)
@@ -145,7 +145,7 @@ def tile_linear_style_blend_k5_kernel(
         rest = keep.tile([P, TILES], F32, name="rest")
 
         def turn_vectors():
-            turned = psum.tile([P, GROUP], F32, name="turned", tag="xt")
+            turned = psum.tile([P, GROUP], F32, name="turned", tag="xt", bufs=BANKS["xt"])
             nc.tensor.transpose(turned[:, 0:P], rows_f32[:], ident[:])
             nc.scalar.copy(out=columns[:], in_=turned[:, 0 : SHIFT_ROW + CHANNELS // P])
 
@@ -176,7 +176,7 @@ def tile_linear_style_blend_k5_kernel(
         z_bank = {}
         u_t = {}
         u_bank = {}
-        y_sb = {}
+        kept = {}
         y_rows = {}
         y_word = {}
         xt_bank = {}
@@ -188,7 +188,7 @@ def tile_linear_style_blend_k5_kernel(
         def stage1(n):
             code_part, code_at = part_of(X_CODE_PARTS, P * n)
             scale_part, scale_at = part_of(X_SCALE_PARTS, P * n)
-            h_bank[n] = psum.tile([P, PACK, P], F32, name="h_bank", tag="h")
+            h_bank[n] = psum.tile([P, PACK, P], F32, name="h_bank", tag="h", bufs=BANKS["h"])
             for t in range(PACK):
                 for g in range(GROUPS):
                     nc.tensor.matmul_mx(
@@ -232,7 +232,7 @@ def tile_linear_style_blend_k5_kernel(
             per_bank = GROUP // width
             for k, j in enumerate(channel_tiles(s)):
                 if k % per_bank == 0:
-                    bank = psum.tile([P, per_bank, width], F32, name="bank", tag="z")
+                    bank = psum.tile([P, per_bank, width], F32, name="bank", tag="z", bufs=BANKS["z"])
                 z_bank[c, j] = bank[:, k % per_bank, :]
                 nc.tensor.matmul_mx(
                     out=z_bank[c, j],
@@ -247,7 +247,7 @@ def tile_linear_style_blend_k5_kernel(
         def add_shift(s):
             c = steps[s][0]
             for j in channel_tiles(s):
-                u_t[c, j] = work.tile([P, PAIR * CHUNK_PAIRS[c]], F32, name="u_t", bufs=10)
+                u_t[c, j] = work.tile([P, PAIR * CHUNK_PAIRS[c]], F32, name="u_t", bufs=12)
                 nc.scalar.activation(
                     out=u_t[c, j][:],
                     in_=z_bank[c, j],
@@ -256,27 +256,26 @@ def tile_linear_style_blend_k5_kernel(
                     scale=1.0,
                 )
 
-        def scale_content(pair):
-            y_pair = work.tile([P, GROUPS, 2, GROUP], F32, name="y_pair", bufs=Y_BUFS)
-            for k in range(2):
+        def scale_content(s):
+            c, g, half = steps[s]
+            pair = first_pair[c] + half
+            for k in reversed(range(2)):
                 n = 2 * pair + k
+                kept[s, k] = work.tile([P, GROUP], F32, name="kept", bufs=2 * SCALE_AHEAD)
                 nc.gpsimd.tensor_scalar(
-                    out=y_pair[:, :, k, :],
-                    in0=content_sb[pair][:, k, :].rearrange("p (g c) -> p g c", g=GROUPS),
+                    out=kept[s, k][:],
+                    in0=content_sb[pair][:, k, GROUP * g : GROUP * (g + 1)],
                     scalar1=rest[:, n : n + 1],
                     scalar2=0.0,
                     op0=ALU.mult,
                     op1=ALU.add,
                 )
-            y_rows[pair] = y_pair
-            for g in range(GROUPS):
-                y_sb[pair, g] = y_pair[:, g, :, :]
 
         def turn_u(s):
             c, g, half = steps[s]
             for k in range(2):
                 at = PAIR * half + P * k
-                u_bank[s, k] = psum.tile([P, GROUP], F32, name="u_bank", tag="u")
+                u_bank[s, k] = psum.tile([P, GROUP], F32, name="u_bank", tag="u", bufs=BANKS["u"])
                 for jj in range(PACK):
                     nc.tensor.transpose(
                         u_bank[s, k][:, P * jj : P * (jj + 1)], u_t[c, PACK * g + jj][:, at : at + P], ident[:]
@@ -285,13 +284,15 @@ def tile_linear_style_blend_k5_kernel(
         def blend(s):
             c, g, half = steps[s]
             pair = first_pair[c] + half
+            if g == 0:
+                y_rows[pair] = work.tile([P, GROUPS, 2, GROUP], F32, name="y_rows", bufs=Y_BUFS)
             for k in range(2):
                 n = 2 * pair + k
                 nc.vector.scalar_tensor_tensor(
-                    out=y_sb[pair, g][:, k, :],
+                    out=y_rows[pair][:, g, k, :],
                     in0=u_bank[s, k][:],
                     scalar=columns[:, n : n + 1],
-                    in1=y_sb[pair, g][:, k, :],
+                    in1=kept[s, k][:],
                     op0=ALU.mult,
                     op1=ALU.add,
                 )
@@ -302,20 +303,20 @@ def tile_linear_style_blend_k5_kernel(
                     )
 
         def round_y(s):
-            y_word[s] = work.tile([P, 2, PAIR, 2], BF16, name="y_word", bufs=3, align_bytes=64)
             c, g, half = steps[s]
-            src = y_sb[first_pair[c] + half, g].rearrange("q k c -> q (k c)").rearrange("q (w u e) -> q u w e", u=2, e=2)
+            y_word[s] = work.tile([P, 2, 2, P, 2], BF16, name="y_word", bufs=3, align_bytes=64)
+            src = y_rows[first_pair[c] + half][:, g, :, :].rearrange("q k (p u e) -> q k u p e", u=2, e=2)
             if s in ROUND_ON_VECTOR:
                 nc.vector.tensor_copy(out=y_word[s][:], in_=src)
             else:
                 nc.scalar.copy(out=y_word[s][:], in_=src)
 
         def turn_y(s):
-            xt_bank[s] = psum.tile([P, 2, 2, P], F32, name="xt_bank", tag="xt")
-            words = y_word[s][:].rearrange("q u w e -> q (u w e)").bitcast(F32)
-            for u in range(2):
-                for k in range(2):
-                    at = P * (2 * u + k)
+            xt_bank[s] = psum.tile([P, 2, 2, P], F32, name="xt_bank", tag="xt", bufs=BANKS["xt"])
+            words = y_word[s][:].rearrange("q k u p e -> q (k u p e)").bitcast(F32)
+            for k in range(2):
+                for u in range(2):
+                    at = P * (2 * k + u)
                     nc.tensor.transpose(xt_bank[s][:, k, u, :], words[:, at : at + P], ident[:])
 
         def gather_words(s):
@@ -329,20 +330,24 @@ def tile_linear_style_blend_k5_kernel(
             else:
                 nc.scalar.copy(out=words[:, half, :, :, :], in_=src)
 
-        def quantize_y(s):
+        def quantize_y(s, count):
             c, g, half = steps[s]
-            lo = PAIR * first_pair[c]
-            hi = lo + PAIR * CHUNK_PAIRS[c]
-            y_code = work.tile([P, hi - lo], U32, name="y_code", bufs=4, align_bytes=64)
-            plane = y_scale[:, g, lo:hi] if lo < tail else y_scale_tail[:, g, :]
-            nc.vector.quantize_mx(out=y_code[:].bitcast(FP8X4), scales=plane, in_=y_in[c, g][:])
-            nc.sync.dma_start(
-                out=out_1[g, :, lo:hi, :].rearrange("p m t -> p (m t)").bitcast(I32), in_=y_code[:].bitcast(I32)
+            at = PAIR * (half + 1 - count)
+            width = PAIR * count
+            lo = PAIR * first_pair[c] + at
+            y_code = work.tile([P, width], U32, name="y_code", bufs=4, align_bytes=64)
+            plane = y_scale[:, g, lo : lo + width] if lo < tail else y_scale_tail[:, g, lo - tail : lo - tail + width]
+            nc.vector.quantize_mx(
+                out=y_code[:].bitcast(FP8X4), scales=plane, in_=y_in[c, g][:, PACK * at : PACK * (at + width)]
             )
-            if g == GROUPS - 1 and c == len(CHUNK_PAIRS) - 2:
-                store_scales(y_scale, 0, hi)
-            if g == GROUPS - 1 and c == len(CHUNK_PAIRS) - 1:
-                store_scales(y_scale_tail, lo, hi)
+            nc.sync.dma_start(
+                out=out_1[g, :, lo : lo + width, :].rearrange("p m t -> p (m t)").bitcast(I32),
+                in_=y_code[:].bitcast(I32),
+            )
+            if g == GROUPS - 1 and lo + width == tail:
+                store_scales(y_scale, 0, tail)
+            if s == STEPS - 1:
+                store_scales(y_scale_tail, tail, PIXELS)
 
         def store_scales(plane, lo, hi):
             for q in range(4):
@@ -352,59 +357,63 @@ def tile_linear_style_blend_k5_kernel(
                 )
 
         def gather_on_vector(s):
-            return s < GATHER_ALL_TO and (s % GATHER_EVERY == 0 or s >= GATHER_ALL_FROM)
+            return s < GATHER_ALL_TO and (s % 2 == 1 or s >= GATHER_ALL_FROM)
 
-        def slot_of(s):
-            return s - HEAD_SHIFT if steps[s][0] == 0 else s
+        def live(s):
+            return 0 <= s < STEPS
 
-        def at_slot(slot):
-            return [s for s in range(STEPS) if slot_of(s) == slot]
+        quantize_slot = [GROUPS * first - 3 for first in first_pair]
+        stage1_slot = []
+        for c, pairs in enumerate(CHUNK_PAIRS):
+            room = GROUPS * CHUNK_PAIRS[max(c - 1, 0)]
+            stage1_slot.extend(quantize_slot[c] - room + i * room // (2 * pairs) for i in range(2 * pairs))
 
-        style_interleave(0)
-        style_interleave(1)
         nc.vector.tensor_copy(
             out=gain_wide[:], in_=gain_sb[:].unsqueeze(1).unsqueeze(3).to_broadcast([P, P // 2, PACK, 2])
         )
+        style_interleave(0)
+        style_interleave(1)
         style_quantize(0)
-        for slot in range(-STAGE1_AHEAD, STEPS + 3):
-            n = slot + STAGE1_AHEAD
-            for s in at_slot(slot + 2):
-                stage2(s)
-            if n < TILES:
+        for slot in range(stage1_slot[0], STEPS + 4):
+            tiles = [n for n in range(TILES) if stage1_slot[n] == slot]
+            if live(slot + 2):
+                stage2(slot + 2)
+            if live(slot):
+                turn_u(slot)
+            if live(slot - 2):
+                turn_y(slot - 2)
+            for n in tiles:
                 stage1(n)
-            if n == 1:
+            if 1 in tiles:
                 turn_vectors()
-            for s in at_slot(slot):
-                turn_u(s)
-            for s in at_slot(slot - 2):
-                turn_y(s)
-            for s in at_slot(slot - 3):
-                if not gather_on_vector(s):
-                    gather_words(s)
-            for s in at_slot(slot + 2):
-                add_shift(s)
-                if s == 0:
-                    nc.scalar.activation(out=rest[:], in_=columns[:, 0:TILES], func=ACT.Copy, scale=-1.0, bias=1.0)
-            for s in at_slot(slot - 1):
-                if s not in ROUND_ON_VECTOR:
-                    round_y(s)
-            if 0 < n <= TILES and n % 2 == 0 and (n == TILES or n // 2 in first_pair):
-                quantize_h(chunk_of_pair[n // 2 - 1])
-            for s in at_slot(slot - 1):
-                if s in ROUND_ON_VECTOR:
-                    round_y(s)
-            for s in at_slot(slot + SCALE_AHEAD):
-                if steps[s][1] == 0:
-                    scale_content(first_pair[steps[s][0]] + steps[s][2])
-            for s in at_slot(slot - 3):
-                if gather_on_vector(s):
-                    gather_words(s)
-            if n < TILES:
-                apply_gain(n)
-            if slot == slot_of(0) - 3:
+
+            if live(slot - 3) and not gather_on_vector(slot - 3):
+                gather_words(slot - 3)
+            if live(slot + 2):
+                add_shift(slot + 2)
+            if slot == REST_SLOT:
+                nc.scalar.activation(out=rest[:], in_=columns[:, 0:TILES], func=ACT.Copy, scale=-1.0, bias=1.0)
+            if live(slot - 1) and slot - 1 not in ROUND_ON_VECTOR:
+                round_y(slot - 1)
+
+            if live(slot - 4):
+                c, g, half = steps[slot - 4]
+                if slot - 4 >= STEPS - 2 * FINE_TAIL:
+                    quantize_y(slot - 4, 1)
+                elif half == CHUNK_PAIRS[c] - 1:
+                    quantize_y(slot - 4, CHUNK_PAIRS[c])
+            if slot in quantize_slot:
+                quantize_h(quantize_slot.index(slot))
+            if slot == quantize_slot[0]:
                 style_quantize(1)
-            for s in at_slot(slot):
-                blend(s)
-            for s in at_slot(slot - 3):
-                if steps[s][2] == CHUNK_PAIRS[steps[s][0]] - 1:
-                    quantize_y(s)
+            if live(slot - 1) and slot - 1 in ROUND_ON_VECTOR:
+                round_y(slot - 1)
+            if live(slot):
+                blend(slot)
+            if live(slot - 3) and gather_on_vector(slot - 3):
+                gather_words(slot - 3)
+            for n in tiles:
+                apply_gain(n)
+
+            if live(slot + SCALE_AHEAD):
+                scale_content(slot + SCALE_AHEAD)

from contextlib import ExitStack

import concourse.mybir as mybir
from concourse.masks import make_identity

F32 = mybir.dt.float32
BF16 = mybir.dt.bfloat16
I32 = mybir.dt.int32
U32 = mybir.dt.uint32
U16 = mybir.dt.uint16
U8 = mybir.dt.uint8
FP8X4 = mybir.dt.float8_e4m3fn_x4
FP4X4 = mybir.dt.float4_e2m1fn_x4
ALU = mybir.AluOpType
ACT = mybir.ActivationFunctionType

PIXELS, CHANNELS, LATENT = 3072, 1024, 512
FLOPS = 2 * PIXELS * CHANNELS * LATENT * 2

P = 128
PACK = 4
GROUP = P * PACK
GROUPS = CHANNELS // GROUP
TILES = PIXELS // P
PAIR = 2 * P
PAIRS = PIXELS // PAIR
CHUNK_PAIRS = [1, 1, 2, 2, 2, 2, 2]
STEPS = GROUPS * PAIRS
SHIFT_ROW = 32
X_CODE_PARTS = [0, 256, 1024, PIXELS]
X_SCALE_PARTS = [0, 1024, PIXELS]
ROUND_ON_VECTOR = [23]
GATHER_ALL_FROM = 16
GATHER_ALL_TO = 19
SCALE_AHEAD = 2
REST_SLOT = -2
FINE_TAIL = 1
BANKS = {"h": 2, "z": 2, "u": 2, "xt": 2}
Y_BUFS = 5


def part_of(bounds, pixel):
    n = max(i for i in range(len(bounds) - 1) if bounds[i] <= pixel)
    return n, pixel - bounds[n]


def tile_linear_style_blend_k5_kernel(
    tc, x_words, x_scales, e_words, e_scales, gain, style, shift, strength, content, out_0, out_1, out_2
):
    nc = tc.nc
    first_pair = [sum(CHUNK_PAIRS[:c]) for c in range(len(CHUNK_PAIRS))]
    steps = [(c, g, half) for c, pairs in enumerate(CHUNK_PAIRS) for g in range(GROUPS) for half in range(pairs)]
    chunk_of_pair = [c for c, pairs in enumerate(CHUNK_PAIRS) for half in range(pairs)]

    with ExitStack() as ctx:
        keep = ctx.enter_context(tc.tile_pool(name="keep", bufs=1))
        work = ctx.enter_context(tc.tile_pool(name="work", bufs=2))
        psum = ctx.enter_context(tc.psum_pool(name="psum", bufs=2))
        ctx.enter_context(tc.manual_schedule())

        def load_scale_rows(plane, scales, lo, hi):
            for q in range(4):
                nc.sync.dma_start(
                    out=plane[32 * q : 32 * q + 4, :, :].bitcast(I32),
                    in_=scales[:, 4 * q : 4 * q + 4, lo:hi].rearrange("g r n -> r g n").bitcast(I32),
                )

        e_scale_raw = keep.tile([P, GROUPS, LATENT], U8, name="e_scale_raw", align_bytes=64)
        nc.vector.memset(e_scale_raw[:].bitcast(I32), 0)
        x_code = {}
        x_scale = {}
        for n in range(len(X_SCALE_PARTS) - 1):
            width = X_SCALE_PARTS[n + 1] - X_SCALE_PARTS[n]
            x_scale[n] = keep.tile([P, GROUPS, width], U8, name="x_scale%d" % n, align_bytes=64)
            nc.vector.memset(x_scale[n][:].bitcast(I32), 0)

        def load_x_codes(n):
            lo, hi = X_CODE_PARTS[n], X_CODE_PARTS[n + 1]
            x_code[n] = keep.tile([P, GROUPS, 2 * (hi - lo)], U8, name="x_code%d" % n, align_bytes=64)
            nc.sync.dma_start(
                out=x_code[n][:].bitcast(I32),
                in_=x_words[:, :, 2 * lo : 2 * hi].rearrange("g p b -> p g b").bitcast(I32),
            )

        def load_x_scales(n):
            load_scale_rows(x_scale[n], x_scales, X_SCALE_PARTS[n], X_SCALE_PARTS[n + 1])

        gain_sb = keep.tile([P, PACK], BF16, name="gain_sb")
        rows_bf = keep.tile([P, P], BF16, name="rows_bf")
        shift_rows = slice(SHIFT_ROW, SHIFT_ROW + CHANNELS // P)
        nc.gpsimd.dma_start(out=rows_bf[0:TILES, :], in_=strength.rearrange("(i p) -> i p", p=P))
        nc.gpsimd.dma_start(out=rows_bf[shift_rows, :], in_=shift.rearrange("(j p) -> j p", p=P))
        rows_f32 = keep.tile([P, P], F32, name="rows_f32")
        nc.gpsimd.memset(rows_f32[:], 0.0)
        ident = keep.tile([P, P], F32, name="ident")
        make_identity(nc, ident[:])
        nc.scalar.copy(out=rows_f32[0:TILES, :], in_=rows_bf[0:TILES, :])
        nc.scalar.copy(out=rows_f32[shift_rows, :], in_=rows_bf[shift_rows, :])

        e_code_raw = keep.tile([P, GROUPS, 2 * LATENT], U8, name="e_code_raw", align_bytes=64)
        style_raw = {}

        def load_style(g):
            style_raw[g] = keep.tile([P, PACK, GROUP], BF16, name="style_raw%d" % g, align_bytes=64)
            nc.sync.dma_start(
                out=style_raw[g][:],
                in_=style[:, GROUP * g : GROUP * (g + 1)].rearrange("(p t) c -> p t c", t=PACK),
            )

        content_sb = {}

        def load_content(pair):
            content_sb[pair] = keep.tile([P, 2, CHANNELS], BF16, name="content%d" % pair)
            nc.sync.dma_start(
                out=content_sb[pair][:],
                in_=content[PAIR * pair : PAIR * (pair + 1), :].rearrange("(i p) c -> p i c", p=P),
            )

        nc.sync.dma_start(out=e_code_raw[:].bitcast(I32), in_=e_words.rearrange("g p b -> p g b").bitcast(I32))
        load_scale_rows(e_scale_raw, e_scales, 0, LATENT)
        load_x_codes(0)
        load_style(0)
        nc.sync.dma_start(out=gain_sb[:], in_=gain.rearrange("(p t) -> p t", t=PACK))
        load_x_scales(0)
        load_style(1)
        load_x_codes(1)
        load_content(0)
        load_content(1)
        load_content(2)
        load_x_scales(1)
        load_x_codes(2)
        for pair in range(3, PAIRS):
            load_content(pair)

        e_code = keep.tile([P, GROUPS, PACK, 2 * P], U8, name="e_code", align_bytes=64)
        e_scale = keep.tile([P, GROUPS, PACK, P], U8, name="e_scale", align_bytes=64)
        nc.vector.tensor_copy(
            out=e_code[:].bitcast(U16),
            in_=e_code_raw[:].bitcast(U16).rearrange("p g (m t) -> p g t m", t=PACK),
        )
        nc.vector.tensor_copy(out=e_scale[:], in_=e_scale_raw[:].rearrange("p g (m t) -> p g t m", t=PACK))

        gain_wide = keep.tile([P, P // 2, PACK, 2], F32, name="gain_wide")
        columns = keep.tile([P, SHIFT_ROW + CHANNELS // P], F32, name="columns")
        rest = keep.tile([P, TILES], F32, name="rest")

        def turn_vectors():
            turned = psum.tile([P, GROUP], F32, name="turned", tag="xt", bufs=BANKS["xt"])
            nc.tensor.transpose(turned[:, 0:P], rows_f32[:], ident[:])
            nc.scalar.copy(out=columns[:], in_=turned[:, 0 : SHIFT_ROW + CHANNELS // P])

        style_code = keep.tile([P, CHANNELS], U32, name="style_code", align_bytes=64)
        style_scale = keep.tile([P, CHANNELS], U8, name="style_scale", align_bytes=64)
        style_in = {}

        def style_interleave(g):
            style_in[g] = keep.tile([P, GROUP, PACK], BF16, name="style_in%d" % g, align_bytes=64)
            dst = style_in[g][:].rearrange("p (c i) t -> p c t i", i=4)
            src = style_raw[g][:].rearrange("p t (c i) -> p c t i", i=4)
            if g == 0:
                nc.vector.tensor_copy(out=dst, in_=src)
            else:
                nc.scalar.copy(out=dst, in_=src)

        def style_quantize(g):
            nc.vector.quantize_mx(
                out=style_code[:, GROUP * g : GROUP * (g + 1)].bitcast(FP8X4),
                scales=style_scale[:, GROUP * g : GROUP * (g + 1)],
                in_=style_in[g][:].rearrange("p c t -> p (c t)"),
            )

        h_bank = {}
        h_in = {}
        h_code = {}
        h_scale = {}
        z_bank = {}
        u_t = {}
        u_bank = {}
        kept = {}
        y_rows = {}
        y_word = {}
        xt_bank = {}
        y_in = {}
        tail = PIXELS - PAIR * CHUNK_PAIRS[-1]
        y_scale = keep.tile([P, GROUPS, tail], U8, name="y_scale", align_bytes=64)
        y_scale_tail = keep.tile([P, GROUPS, PIXELS - tail], U8, name="y_scale_tail", align_bytes=64)

        def stage1(n):
            code_part, code_at = part_of(X_CODE_PARTS, P * n)
            scale_part, scale_at = part_of(X_SCALE_PARTS, P * n)
            h_bank[n] = psum.tile([P, PACK, P], F32, name="h_bank", tag="h", bufs=BANKS["h"])
            for t in range(PACK):
                for g in range(GROUPS):
                    nc.tensor.matmul_mx(
                        out=h_bank[n][:, t, :],
                        lhsT=e_code[:, g, t, :].bitcast(FP4X4),
                        lhsT_scale=e_scale[:, g, t, :],
                        rhs=x_code[code_part][:, g, 2 * code_at : 2 * (code_at + P)].bitcast(FP4X4),
                        rhs_scale=x_scale[scale_part][:, g, scale_at : scale_at + P],
                        start=(g == 0),
                        stop=(g == GROUPS - 1),
                    )

        def apply_gain(n):
            c = chunk_of_pair[n // 2]
            i = n - 2 * first_pair[c]
            if i == 0:
                h_in[c] = work.tile([P, PAIR * CHUNK_PAIRS[c], PACK], BF16, name="h_in", align_bytes=64)
            nc.vector.tensor_tensor(
                out=h_in[c][:, P * i : P * (i + 1), :].rearrange("p (m i) t -> p m t i", i=2),
                in0=h_bank[n][:].rearrange("p t (m i) -> p m t i", i=2),
                in1=gain_wide[:],
                op=ALU.mult,
            )

        def quantize_h(c):
            width = PAIR * CHUNK_PAIRS[c]
            h_code[c] = work.tile([P, width], U32, name="h_code", align_bytes=64)
            h_scale[c] = work.tile([P, width], U8, name="h_scale", align_bytes=64)
            nc.vector.quantize_mx(
                out=h_code[c][:].bitcast(FP8X4), scales=h_scale[c][:], in_=h_in[c][:].rearrange("p n t -> p (n t)")
            )

        def channel_tiles(s):
            c, g, half = steps[s]
            count = PACK // CHUNK_PAIRS[c]
            return [PACK * g + count * half + k for k in range(count)]

        def stage2(s):
            c = steps[s][0]
            width = PAIR * CHUNK_PAIRS[c]
            per_bank = GROUP // width
            for k, j in enumerate(channel_tiles(s)):
                if k % per_bank == 0:
                    bank = psum.tile([P, per_bank, width], F32, name="bank", tag="z", bufs=BANKS["z"])
                z_bank[c, j] = bank[:, k % per_bank, :]
                nc.tensor.matmul_mx(
                    out=z_bank[c, j],
                    lhsT=style_code[:, P * j : P * (j + 1)].bitcast(FP8X4),
                    lhsT_scale=style_scale[:, P * j : P * (j + 1)],
                    rhs=h_code[c][:].bitcast(FP8X4),
                    rhs_scale=h_scale[c][:],
                    start=True,
                    stop=True,
                )

        def add_shift(s):
            c = steps[s][0]
            for j in channel_tiles(s):
                u_t[c, j] = work.tile([P, PAIR * CHUNK_PAIRS[c]], F32, name="u_t", bufs=12)
                nc.scalar.activation(
                    out=u_t[c, j][:],
                    in_=z_bank[c, j],
                    func=ACT.Identity,
                    bias=columns[:, SHIFT_ROW + j : SHIFT_ROW + j + 1],
                    scale=1.0,
                )

        def scale_content(s):
            c, g, half = steps[s]
            pair = first_pair[c] + half
            for k in reversed(range(2)):
                n = 2 * pair + k
                kept[s, k] = work.tile([P, GROUP], F32, name="kept", bufs=2 * SCALE_AHEAD)
                nc.gpsimd.tensor_scalar(
                    out=kept[s, k][:],
                    in0=content_sb[pair][:, k, GROUP * g : GROUP * (g + 1)],
                    scalar1=rest[:, n : n + 1],
                    scalar2=0.0,
                    op0=ALU.mult,
                    op1=ALU.add,
                )

        def turn_u(s):
            c, g, half = steps[s]
            for k in range(2):
                at = PAIR * half + P * k
                u_bank[s, k] = psum.tile([P, GROUP], F32, name="u_bank", tag="u", bufs=BANKS["u"])
                for jj in range(PACK):
                    nc.tensor.transpose(
                        u_bank[s, k][:, P * jj : P * (jj + 1)], u_t[c, PACK * g + jj][:, at : at + P], ident[:]
                    )

        def blend(s):
            c, g, half = steps[s]
            pair = first_pair[c] + half
            if g == 0:
                y_rows[pair] = work.tile([P, GROUPS, 2, GROUP], F32, name="y_rows", bufs=Y_BUFS)
            for k in range(2):
                n = 2 * pair + k
                nc.vector.scalar_tensor_tensor(
                    out=y_rows[pair][:, g, k, :],
                    in0=u_bank[s, k][:],
                    scalar=columns[:, n : n + 1],
                    in1=kept[s, k][:],
                    op0=ALU.mult,
                    op1=ALU.add,
                )
                if g == GROUPS - 1:
                    nc.sync.dma_start(
                        out=out_0[P * n : P * (n + 1), :].rearrange("p (g c) -> p g c", g=GROUPS),
                        in_=y_rows[pair][:, :, k, :],
                    )

        def round_y(s):
            c, g, half = steps[s]
            y_word[s] = work.tile([P, 2, 2, P, 2], BF16, name="y_word", bufs=3, align_bytes=64)
            src = y_rows[first_pair[c] + half][:, g, :, :].rearrange("q k (p u e) -> q k u p e", u=2, e=2)
            if s in ROUND_ON_VECTOR:
                nc.vector.tensor_copy(out=y_word[s][:], in_=src)
            else:
                nc.scalar.copy(out=y_word[s][:], in_=src)

        def turn_y(s):
            xt_bank[s] = psum.tile([P, 2, 2, P], F32, name="xt_bank", tag="xt", bufs=BANKS["xt"])
            words = y_word[s][:].rearrange("q k u p e -> q (k u p e)").bitcast(F32)
            for k in range(2):
                for u in range(2):
                    at = P * (2 * k + u)
                    nc.tensor.transpose(xt_bank[s][:, k, u, :], words[:, at : at + P], ident[:])

        def gather_words(s):
            c, g, half = steps[s]
            if half == 0:
                y_in[c, g] = work.tile([P, PAIR * CHUNK_PAIRS[c] * PACK], BF16, name="y_in", bufs=3, align_bytes=64)
            words = y_in[c, g][:].bitcast(F32).rearrange("p (h k r u) -> p h k r u", k=2, r=P, u=2)
            src = xt_bank[s][:].rearrange("p k u r -> p k r u")
            if gather_on_vector(s):
                nc.vector.tensor_copy(out=words[:, half, :, :, :], in_=src)
            else:
                nc.scalar.copy(out=words[:, half, :, :, :], in_=src)

        def quantize_y(s, count):
            c, g, half = steps[s]
            at = PAIR * (half + 1 - count)
            width = PAIR * count
            lo = PAIR * first_pair[c] + at
            y_code = work.tile([P, width], U32, name="y_code", bufs=4, align_bytes=64)
            plane = y_scale[:, g, lo : lo + width] if lo < tail else y_scale_tail[:, g, lo - tail : lo - tail + width]
            nc.vector.quantize_mx(
                out=y_code[:].bitcast(FP8X4), scales=plane, in_=y_in[c, g][:, PACK * at : PACK * (at + width)]
            )
            nc.sync.dma_start(
                out=out_1[g, :, lo : lo + width, :].rearrange("p m t -> p (m t)").bitcast(I32),
                in_=y_code[:].bitcast(I32),
            )
            if g == GROUPS - 1 and lo + width == tail:
                store_scales(y_scale, 0, tail)
            if s == STEPS - 1:
                store_scales(y_scale_tail, tail, PIXELS)

        def store_scales(plane, lo, hi):
            for q in range(4):
                nc.sync.dma_start(
                    out=out_2[:, 4 * q : 4 * q + 4, lo:hi].rearrange("g r m -> r g m").bitcast(I32),
                    in_=plane[32 * q : 32 * q + 4, :, :].bitcast(I32),
                )

        def gather_on_vector(s):
            return s < GATHER_ALL_TO and (s % 2 == 1 or s >= GATHER_ALL_FROM)

        def live(s):
            return 0 <= s < STEPS

        quantize_slot = [GROUPS * first - 3 for first in first_pair]
        stage1_slot = []
        for c, pairs in enumerate(CHUNK_PAIRS):
            room = GROUPS * CHUNK_PAIRS[max(c - 1, 0)]
            stage1_slot.extend(quantize_slot[c] - room + i * room // (2 * pairs) for i in range(2 * pairs))

        nc.vector.tensor_copy(
            out=gain_wide[:], in_=gain_sb[:].unsqueeze(1).unsqueeze(3).to_broadcast([P, P // 2, PACK, 2])
        )
        style_interleave(0)
        style_interleave(1)
        style_quantize(0)
        for slot in range(stage1_slot[0], STEPS + 4):
            tiles = [n for n in range(TILES) if stage1_slot[n] == slot]
            if live(slot + 2):
                stage2(slot + 2)
            if live(slot):
                turn_u(slot)
            if live(slot - 2):
                turn_y(slot - 2)
            for n in tiles:
                stage1(n)
            if 1 in tiles:
                turn_vectors()

            if live(slot - 3) and not gather_on_vector(slot - 3):
                gather_words(slot - 3)
            if live(slot + 2):
                add_shift(slot + 2)
            if slot == REST_SLOT:
                nc.scalar.activation(out=rest[:], in_=columns[:, 0:TILES], func=ACT.Copy, scale=-1.0, bias=1.0)
            if live(slot - 1) and slot - 1 not in ROUND_ON_VECTOR:
                round_y(slot - 1)

            if live(slot - 4):
                c, g, half = steps[slot - 4]
                if slot - 4 >= STEPS - 2 * FINE_TAIL:
                    quantize_y(slot - 4, 1)
                elif half == CHUNK_PAIRS[c] - 1:
                    quantize_y(slot - 4, CHUNK_PAIRS[c])
            if slot in quantize_slot:
                quantize_h(quantize_slot.index(slot))
            if slot == quantize_slot[0]:
                style_quantize(1)
            if live(slot - 1) and slot - 1 in ROUND_ON_VECTOR:
                round_y(slot - 1)
            if live(slot):
                blend(slot)
            if live(slot - 3) and gather_on_vector(slot - 3):
                gather_words(slot - 3)
            for n in tiles:
                apply_gain(n)

            if live(slot + SCALE_AHEAD):
                scale_content(slot + SCALE_AHEAD)
